import numpy as np
import ml_dtypes


def mxq(x, axis, fmt="e4m3"):
    dtype, down = {"e4m3": (ml_dtypes.float8_e4m3fn, 7), "e5m2": (ml_dtypes.float8_e5m2, 14)}[fmt]
    v = np.moveaxis(np.asarray(x, np.float32).astype(ml_dtypes.bfloat16).astype(np.float64), axis, -1)
    blocks = v.reshape(v.shape[:-1] + (-1, 32))
    amax = np.abs(blocks).max(-1, keepdims=True)
    byte = np.maximum(np.where(amax > 0, np.frexp(amax)[1] - 1 + 127, 0) - down, 1)
    scale = np.exp2(byte - 127.0)
    codes = (blocks / scale).astype(np.float32).astype(dtype).astype(np.float64)
    return np.moveaxis((codes * scale).reshape(v.shape), -1, axis)


WIDE = False


def mx_kscale(k):
    if not WIDE:
        return np.ones(k)
    levels = np.array([10, -10, 5, -5, 0])
    if k % 512:
        return np.exp2(np.random.permutation(np.resize(levels, k // 32))).repeat(32)
    a = np.empty((k // 512, 16))
    for p in range(k // 512):
        a[p, :8] = np.random.permutation(np.resize(levels, 8))
        for g in range(8):
            far = levels[np.abs(levels - a[p, g]) >= 10]
            a[p, g + 8] = far[np.random.randint(len(far))]
    return np.exp2(a.ravel()).repeat(32)


def f64(x):
    return np.asarray(x).astype(np.float64)


def striped(idx):
    return np.tile(idx.reshape(-1, 16).T, (8, 1)).astype(np.uint16)


def unstriped(offs):
    return offs[:16].T.reshape(-1).astype(np.int64)


def sigmoid(v):
    return 1.0 / (1.0 + np.exp(-np.maximum(v, -700.0)))


K, T, E, C, H, N = 1024, 1024, 4, 128, 512, 128


def by_expert(wq, xq):
    return np.concatenate([wq[e].T @ xq[:, e * C:(e + 1) * C] for e in range(E)], axis=1)


def setup_inputs():
    n = np.random.standard_normal
    s = mx_kscale(K)[:, None]
    u = mx_kscale(H)
    return {
        "xT": (n((K, T)) * s).astype(np.float32),
        "w1": (n((E + 1, K, H)) / np.sqrt(K) / s[None]).astype(np.float32),
        "w3": (n((E + 1, K, H)) / np.sqrt(K) / s[None] * u[None, None, :]).astype(np.float32),
        "w2": (n((E + 1, H, N)) / np.sqrt(H) / u[None, :, None]).astype(np.float32),
        "gate": np.tile(np.random.uniform(0.2, 1.0, E * C), (N, 1)).astype(np.float32),
        "offs": striped(np.random.permutation(T)[:E * C]),
    }


def reference(xT, w1, w3, w2, gate, offs):
    idx = unstriped(offs)
    w1q, w3q, w2q = mxq(f64(w1), 1, "e4m3"), mxq(f64(w3), 1, "e4m3"), mxq(f64(w2), 1, "e4m3")
    xs = mxq(f64(xT), 0, "e4m3")
    hs = sigmoid(w1q[E].T @ xs) * (w3q[E].T @ xs)
    ys = w2q[E].T @ mxq(hs, 0, "e4m3")
    xq = mxq(f64(xT)[:, idx], 0, "e4m3")
    h = sigmoid(by_expert(w1q, xq))
    h = h * by_expert(w3q, xq)
    y = by_expert(w2q, mxq(h, 0, "e4m3"))
    out = ys
    out[:, idx] += f64(gate) * y
    return out

from contextlib import ExitStack

import concourse.mybir as mybir

F32 = mybir.dt.float32
BF16 = mybir.dt.bfloat16
I32 = mybir.dt.int32
U32 = mybir.dt.uint32
U16 = mybir.dt.uint16
U8 = mybir.dt.uint8
FP8X4 = mybir.dt.float8_e4m3fn_x4
MULT = mybir.AluOpType.mult
ADD = mybir.AluOpType.add
SIGMOID = mybir.ActivationFunctionType.Sigmoid

P = 128
PACK = 4
K, T, E, C, H, N = 1024, 1024, 4, 128, 512, 128
K_PASS = P * PACK
PASSES = K // K_PASS
SLOTS = E * C
SHARED = E
FLOPS = 2 * (T + SLOTS) * (2 * K * H + H * N)

RAW_BUFS = 9
MS = {SHARED: 116, 0: 108, 1: 92, 2: 92, 3: 88}
MS_LAST = 44
X_S = {(0, 0): 384, (0, 1): 384, (1, 0): 1024, (1, 1): 1024}


def tile_moe_shr_glu_sigmoid_kernel(tc, xT, w1, w3, w2, gate, offs, out):
    nc = tc.nc
    with ExitStack() as ctx:
        keep = ctx.enter_context(tc.tile_pool(name="keep", bufs=1))
        raws = ctx.enter_context(tc.tile_pool(name="raws", bufs=RAW_BUFS))
        work = ctx.enter_context(tc.tile_pool(name="work", bufs=3))
        psum = ctx.enter_context(tc.psum_pool(name="psum", bufs=1))

        offsets = keep.tile([P, SLOTS // 16], U16, name="offsets")
        gate_sb = keep.tile([P, SLOTS], F32, name="gate_sb")
        routed = keep.tile([P, T], F32, name="routed")
        ys_sb = keep.tile([P, T], F32, name="ys_sb")
        warm = keep.tile([P, 1], F32, name="warm")
        xs_codes = keep.tile([P, PASSES, T], U32, name="xs_codes", align_bytes=64)
        xs_scales = keep.tile([P, PASSES, T], U8, name="xs_scales", align_bytes=64)
        xg_codes = keep.tile([P, PASSES, SLOTS], U32, name="xg_codes", align_bytes=64)
        xg_scales = keep.tile([P, PASSES, SLOTS], U8, name="xg_scales", align_bytes=64)

        order = []
        for c in range(PASSES):
            for u in range(2):
                order.append(("x", c, u))
        for e in [SHARED] + list(range(E)):
            for w in ("w1", "w3"):
                for c in range(PASSES):
                    order.append((w, e, c))
        raw = {}
        w2_raw = {}

        def load(i):
            kind, a, b = order[i]
            if kind == "x":
                t = raws.tile([P, 2, T], F32, name="raw_x", tag="raw")
                src = xT[a * K_PASS : (a + 1) * K_PASS, :].rearrange("(p u e) t -> u p e t", u=2, e=2)[b]
            else:
                t = raws.tile([P, PACK, H], F32, name="raw_w", tag="raw")
                src = (w1 if kind == "w1" else w3)[a, b * K_PASS : (b + 1) * K_PASS, :].rearrange("(p j) c -> p j c", j=PACK)
            nc.sync.dma_start(out=t[:], in_=src)
            raw[order[i]] = t
            if i == 0:
                nc.sync.dma_start(offsets[:], offs)
            if kind == "w3" and b == 1:
                load_w2(a)
            if kind == "w3" and a == 0 and b == 1:
                nc.sync.dma_start(out=gate_sb[:], in_=gate)

        def load_w2(e):
            t2 = work.tile([P, PACK, N], F32, name="w2_raw", tag="w2_raw")
            nc.sync.dma_start(out=t2[:], in_=w2[e].rearrange("(p j) n -> p j n", j=PACK))
            w2_raw[e] = t2

        nc.vector.memset(warm[:], 0.0)
        nc.scalar.activation(warm[:], warm[:], SIGMOID)
        nc.vector.memset(routed[:], 0.0)

        pairs = {}
        grouped = {}
        codes = {}
        scales = {}

        def cast_x(c, u):
            if u == 0:
                pairs[c] = work.tile([P, 2, T, 2], BF16, name="pairs", tag="pairs", bufs=2, align_bytes=64)
            src = raw["x", c, u][:].rearrange("p e t -> p t e")
            dst = pairs[c][:, u]
            if X_S[c, u] > 0:
                nc.scalar.copy(out=dst[:, :X_S[c, u]], in_=src[:, :X_S[c, u]])
            if X_S[c, u] < T:
                nc.vector.tensor_copy(out=dst[:, X_S[c, u]:], in_=src[:, X_S[c, u]:])

        def gather_x(c, u, g):
            flat = g[:].rearrange("p s j -> p (s j)").bitcast(U32).rearrange("p (s u) -> p s u", u=2)
            window = pairs[c][:, u].rearrange("p t e -> p (t e)").bitcast(U32)
            nc.vector.tensor_copy(out=flat[:, :, u], in_=window.indirect(offsets[:]))

        def quads_x(c):
            q = work.tile([P, T, PACK], BF16, name="quads", tag="quads", bufs=2, align_bytes=64)
            dst = q[:].rearrange("p t j -> p (t j)").bitcast(I32).rearrange("p (t u) -> p t u", u=2)
            src = pairs[c][:].rearrange("p u t e -> p (u t e)").bitcast(I32).rearrange("p (u t) -> p t u", u=2)
            nc.vector.tensor_copy(out=dst, in_=src)
            return q

        def quant(codes_ap, scales_ap, values):
            nc.vector.quantize_mx(out=codes_ap.bitcast(FP8X4), scales=scales_ap, in_=values)

        def cast_w(key, ms):
            g = work.tile([P, PACK * H], BF16, name="w_grouped", tag="w_grouped", bufs=4, align_bytes=64)
            src = raw[key][:].rearrange("p j (m t) -> p m j t", t=PACK)
            dst = g[:].rearrange("p (t m j) -> p m j t", t=PACK, j=PACK)
            if ms > 0:
                nc.scalar.copy(out=dst[:, :ms], in_=src[:, :ms])
            if ms < P:
                nc.vector.tensor_copy(out=dst[:, ms:], in_=src[:, ms:])
            grouped[key] = g

        def quant_w(key):
            cd = work.tile([P, H], U32, name="w_codes", tag="w_codes", bufs=10, align_bytes=64)
            sc = work.tile([P, H], U8, name="w_scales", tag="w_scales", bufs=10, align_bytes=64)
            parts = 2 if key[1] == E - 1 and key[0] == "w3" and key[2] == 1 else 1
            for i in range(parts):
                s = slice(i * H // parts, (i + 1) * H // parts)
                quant(cd[:, s], sc[:, s], grouped[key][:, s.start * PACK : s.stop * PACK])
            codes[key] = cd
            scales[key] = sc

        def prep_w2(e):
            g = work.tile([P, N, PACK], BF16, name="w2_grouped", tag="w2_grouped", bufs=2, align_bytes=64)
            nc.vector.tensor_copy(out=g[:], in_=w2_raw[e][:].rearrange("p j n -> p n j"))
            cd = work.tile([P, N], U32, name="w2_codes", tag="w2_codes", bufs=3, align_bytes=64)
            sc = work.tile([P, N], U8, name="w2_scales", tag="w2_scales", bufs=3, align_bytes=64)
            quant(cd[:], sc[:], g[:].rearrange("p n j -> p (n j)"))
            codes["w2", e] = cd
            scales["w2", e] = sc

        def layer1(w, e, x_codes, x_scales, cols):
            bank = psum.tile([P, PACK, P], F32, name="bank_" + w, tag=w, bufs=3)
            for t in range(PACK):
                for c in range(PASSES):
                    nc.tensor.matmul_mx(
                        out=bank[:, t, :],
                        lhsT=codes[w, e, c][:, t * P : (t + 1) * P].bitcast(FP8X4),
                        lhsT_scale=scales[w, e, c][:, t * P : (t + 1) * P],
                        rhs=x_codes[:, c, cols].bitcast(FP8X4),
                        rhs_scale=x_scales[:, c, cols],
                        start=(c == 0),
                        stop=(c == PASSES - 1),
                    )
            return bank

        def sigm(bank_a):
            sg = work.tile([P, P, PACK], F32, name="sg", tag="sg", bufs=3)
            nc.scalar.activation(sg[:], bank_a[:].rearrange("p t n -> p n t"), SIGMOID)
            return sg

        def product(sg, bank_b):
            h = work.tile([P, P, PACK], BF16, name="h", tag="h", bufs=3, align_bytes=64)
            nc.vector.tensor_tensor(h[:], sg[:], bank_b[:].rearrange("p t n -> p n t"), MULT)
            return h

        def layer2(e, h_codes, h_scales, n):
            y = psum.tile([P, n], F32, name="y", tag="y", bufs=2)
            nc.tensor.matmul_mx(
                out=y[:],
                lhsT=codes["w2", e][:].bitcast(FP8X4),
                lhsT_scale=scales["w2", e][:],
                rhs=h_codes.bitcast(FP8X4),
                rhs_scale=h_scales,
                start=True,
                stop=True,
            )
            return y

        state = {"next": 0}

        def more_loads(done):
            while state["next"] < len(order) and state["next"] < done + RAW_BUFS:
                load(state["next"])
                state["next"] += 1

        more_loads(0)
        for c in range(PASSES):
            g = work.tile([P, SLOTS, PACK], BF16, name="gathered", tag="gathered", bufs=2, align_bytes=64)
            for u in range(2):
                cast_x(c, u)
                gather_x(c, u, g)
                more_loads(2 * c + u + 1)
            q = quads_x(c)
            quant(xs_codes[:, c, :], xs_scales[:, c, :], q[:].rearrange("p t j -> p (t j)"))
            quant(xg_codes[:, c, :], xg_scales[:, c, :], g[:].rearrange("p s j -> p (s j)"))

        hs_codes = [None, None]
        hs_scales = [None, None]

        def shared_unit(k):
            half, part = divmod(k, 4)
            if part == 0:
                hs_codes[half] = work.tile([P, 4 * P], U32, name="hs_codes", tag="hs_codes", bufs=2, align_bytes=64)
                hs_scales[half] = work.tile([P, 4 * P], U8, name="hs_scales", tag="hs_scales", bufs=2, align_bytes=64)
            cols = slice(k * P, (k + 1) * P)
            a = layer1("w1", SHARED, xs_codes, xs_scales, cols)
            b = layer1("w3", SHARED, xs_codes, xs_scales, cols)
            h = product(sigm(a), b)
            quant(hs_codes[half][:, part * P : (part + 1) * P], hs_scales[half][:, part * P : (part + 1) * P], h[:].rearrange("p n t -> p (n t)"))
            if part == 3:
                y = layer2(SHARED, hs_codes[half][:], hs_scales[half][:], 4 * P)
                nc.scalar.copy(out=ys_sb[:, half * 4 * P : (half + 1) * 4 * P], in_=y[:])

        i = 4
        for n_e, e in enumerate([SHARED] + list(range(E))):
            last = e == E - 1
            for w in ("w1", "w3"):
                for c in range(PASSES):
                    key = (w, e, c)
                    cast_w(key, MS_LAST if last and w == "w3" else MS[e])
                    if n_e == 1:
                        j = (2 if w == "w3" else 0) + c
                        shared_unit(2 * j)
                        shared_unit(2 * j + 1)
                    quant_w(key)
                    i += 1
                    more_loads(i)
                if w == "w1" and e != SHARED:
                    cols = slice(e * C, (e + 1) * C)
                    sg = sigm(layer1("w1", e, xg_codes, xg_scales, cols))
            prep_w2(e)
            if e != SHARED:
                b = layer1("w3", e, xg_codes, xg_scales, cols)
                h = product(sg, b)
                hc = work.tile([P, C], U32, name="h_codes", tag="h_codes", bufs=2, align_bytes=64)
                hsc = work.tile([P, C], U8, name="h_scales", tag="h_scales", bufs=2, align_bytes=64)
                quant(hc[:], hsc[:], h[:].rearrange("p n t -> p (n t)"))
                y = layer2(e, hc[:], hsc[:], C)
                y_sb = work.tile([P, C], F32, name="y_sb", tag="y_sb", bufs=2)
                nc.scalar.copy(out=y_sb[:], in_=y[:])
                nc.vector.tensor_tensor(
                    routed[:].indirect(offsets[:, e * C // 16 : (e + 1) * C // 16]), y_sb[:], gate_sb[:, cols], MULT
                )

        for q in range(4):
            w = T // 4
            o = work.tile([P, w], F32, name="o", tag="o", bufs=4)
            s = slice(q * w, (q + 1) * w)
            nc.vector.tensor_tensor(o[:], ys_sb[:, s], routed[:, s], ADD)
            (nc.sync if q % 2 == 0 else nc.scalar).dma_start(out=out[:, s], in_=o[:])
